import numpy as np
import ml_dtypes


def mxq(x, axis, fmt="e4m3"):
    dtype, down = {"e4m3": (ml_dtypes.float8_e4m3fn, 7), "e5m2": (ml_dtypes.float8_e5m2, 14)}[fmt]
    v = np.moveaxis(np.asarray(x, np.float32).astype(ml_dtypes.bfloat16).astype(np.float64), axis, -1)
    blocks = v.reshape(v.shape[:-1] + (-1, 32))
    amax = np.abs(blocks).max(-1, keepdims=True)
    byte = np.maximum(np.where(amax > 0, np.frexp(amax)[1] - 1 + 127, 0) - down, 1)
    scale = np.exp2(byte - 127.0)
    codes = (blocks / scale).astype(np.float32).astype(dtype).astype(np.float64)
    return np.moveaxis((codes * scale).reshape(v.shape), -1, axis)


WIDE = False


def mx_kscale(k):
    if not WIDE:
        return np.ones(k)
    levels = np.array([10, -10, 5, -5, 0])
    if k % 512:
        return np.exp2(np.random.permutation(np.resize(levels, k // 32))).repeat(32)
    a = np.empty((k // 512, 16))
    for p in range(k // 512):
        a[p, :8] = np.random.permutation(np.resize(levels, 8))
        for g in range(8):
            far = levels[np.abs(levels - a[p, g]) >= 10]
            a[p, g + 8] = far[np.random.randint(len(far))]
    return np.exp2(a.ravel()).repeat(32)


def f64(x):
    return np.asarray(x).astype(np.float64)


def striped(idx):
    return np.tile(idx.reshape(-1, 16).T, (8, 1)).astype(np.uint16)


def unstriped(offs):
    return offs[:16].T.reshape(-1).astype(np.int64)


def striped8(idx):
    return np.concatenate([x.reshape(-1, 16).T for x in idx]).astype(np.uint16)


def runs(offs, k):
    lists = np.stack([offs[16 * r : 16 * r + 16].T.reshape(-1) for r in range(8)]).astype(np.int64)
    return lists[np.arange(k) % 512 // 64]


def pack_weight(w):
    k, n = w.shape
    w = f64(np.asarray(w, np.float32).astype(ml_dtypes.bfloat16)).reshape(k // 32, 32, n)
    amax = np.abs(w).max(1)
    byte = np.clip(np.where(amax > 0, np.frexp(amax)[1] - 1 + 127 - 7, 1), 1, 254)
    scaled = (w * np.exp2(127.0 - byte)[:, None, :]).reshape(k, n).astype(np.float32)
    words = np.ascontiguousarray(scaled.reshape(k // 512, 128, 4, n).transpose(0, 1, 3, 2)).astype(ml_dtypes.float8_e4m3fn).view(np.uint8)
    return words, np.ascontiguousarray(byte.astype(np.uint8).reshape(k // 512, 16, n))


def unpack_weight(words, scales):
    g, p, n, _ = words.shape
    vals = np.ascontiguousarray(words).view(ml_dtypes.float8_e4m3fn).astype(np.float64) * np.repeat(np.exp2(scales.astype(np.float64) - 127.0), 8, axis=1)[..., None]
    return vals.transpose(0, 1, 3, 2).reshape(g * 512, n)


def sigmoid(v):
    return 1.0 / (1.0 + np.exp(-np.maximum(v, -700.0)))


K, T, S, G, H, W, U = 512, 2048, 512, 2048, 512, 1024, 256


def setup_inputs():
    n = np.random.standard_normal
    s = mx_kscale(K)[:, None]
    u = mx_kscale(S)
    packed_xT = pack_weight(n((K, T)) * s)
    packed_dT = pack_weight(n((K, G)) / s)
    perm = np.random.permutation(S)
    return {
        "x_words": packed_xT[0],
        "x_scales": packed_xT[1],
        "d_words": packed_dT[0],
        "d_scales": packed_dT[1],
        "ga": (np.random.uniform(0.5, 1.5, (H, 1)) * u[:, None]).astype(np.float32),
        "gb": (np.random.uniform(0.5, 1.5, (H, 1)) / u[:, None]).astype(np.float32),
        "offs": striped(np.random.permutation(T)[:S]),
        "kidx": striped8(np.random.randint(0, G, (8, H))),
        "n1": striped(np.random.randint(0, S, W)),
        "n2": striped8(np.stack([np.random.permutation(S) for _ in range(8)])),
        "n3": striped8(np.stack([np.random.permutation(S) for _ in range(8)])),
        "n4": striped(perm[:U]),
        "n5": striped(perm[U:]),
    }


def reference(x_words, x_scales, d_words, d_scales, ga, gb, offs, kidx, n1, n2, n3, n4, n5):
    d_kidx = unpack_weight(d_words, d_scales)[np.arange(K)[:, None], runs(kidx, K)]
    xq = unpack_weight(x_words, x_scales)[:, unstriped(offs)]
    s = 0.0625 * (d_kidx.T @ xq)
    mb = s[:, unstriped(n1)]
    ms = mb.reshape(H, S, 2).sum(axis=2)
    mx = mb.reshape(H, S, 2).max(axis=2)
    z = f64(ga) * (ms - np.maximum(s, mx))
    z2 = f64(gb) * (s * (s[np.arange(H)[:, None], runs(n2, H)] - (s[np.arange(H)[:, None], runs(n3, H)])))
    cm = 0.0625 * ((mxq(z, 0, "e4m3").T @ mxq(z2, 0, "e4m3")))
    pa = cm[:, unstriped(n4)]
    pb = cm[:, unstriped(n5)]
    ra = pa * sigmoid(pb)
    out = cm.copy()
    out[:, unstriped(n5)] = ra
    return out

@@ -1,0 +1,243 @@
+from contextlib import ExitStack
+
+import concourse.mybir as mybir
+
+F32 = mybir.dt.float32
+BF16 = mybir.dt.bfloat16
+I32 = mybir.dt.int32
+U32 = mybir.dt.uint32
+U16 = mybir.dt.uint16
+U8 = mybir.dt.uint8
+FP8X4 = mybir.dt.float8_e4m3fn_x4
+ALU = mybir.AluOpType
+ACT = mybir.ActivationFunctionType
+
+P = 128
+PACK = 4
+TABLE = 2048
+S = 512
+PAIRS = 256
+SIXTEENTH = 0.0625
+FLOPS = 2 * 2 * 512 * 512 * 512
+
+
+def tile_picked_simkgpairwindfold_none_p_kernel(
+    tc, x_words, x_scales, d_words, d_scales, ga, gb, offs, kidx, n1, n2, n3, n4, n5, out
+):
+    nc = tc.nc
+    with ExitStack() as ctx:
+        keep = ctx.enter_context(tc.tile_pool(name="keep", bufs=1))
+        psum = ctx.enter_context(tc.psum_pool(name="psum", bufs=1))
+
+        def sb(name, cols, dtype, tag=None):
+            return keep.tile([P, cols], dtype, name=name, tag=tag or name, align_bytes=64)
+
+        def load_list(name, src):
+            t = keep.tile(list(src.shape), U16, name=name)
+            nc.sync.dma_start(t[:], src)
+            return t
+
+        d_scale_table = sb("d_scale_table", TABLE, U8)
+        x_scale_table = sb("x_scale_table", TABLE, U8)
+        for table in (d_scale_table, x_scale_table):
+            nc.vector.memset(table[:, 0 : TABLE // 2].bitcast(I32), 0)
+            nc.gpsimd.memset(table[:, TABLE // 2 :].bitcast(I32), 0)
+        d_word_table = sb("d_word_table", TABLE, I32)
+        x_word_table = sb("x_word_table", TABLE, I32)
+        ga_t = sb("ga_t", PACK, F32)
+        gb_t = sb("gb_t", PACK, F32)
+        kidx_t = load_list("kidx_t", kidx)
+        offs_t = load_list("offs_t", offs)
+        n3_t = load_list("n3_t", n3)
+        n2_t = load_list("n2_t", n2)
+        nc.sync.dma_start(gb_t[:], gb.rearrange("(p t) o -> p (t o)", t=PACK))
+        nc.sync.dma_start(d_scale_table[0:P:8, :].bitcast(I32), d_scales[0].bitcast(I32))
+        nc.sync.dma_start(x_scale_table[0:P:8, :].bitcast(I32), x_scales[0].bitcast(I32))
+        nc.sync.dma_start(d_word_table[:], d_words[0].rearrange("p n t -> p (n t)").bitcast(I32))
+        nc.sync.dma_start(x_word_table[:], x_words[0].rearrange("p n t -> p (n t)").bitcast(I32))
+        n1_t = load_list("n1_t", n1)
+        nc.sync.dma_start(ga_t[:], ga.rearrange("(p t) o -> p (t o)", t=PACK))
+        n5_t = load_list("n5_t", n5)
+        n4_t = load_list("n4_t", n4)
+
+        zero = sb("zero", 1, F32)
+        nc.vector.memset(zero[:], 0.0)
+        s_win = [sb("s_win%d" % t, 2 * S, F32) for t in range(PACK)]
+        for t in range(PACK):
+            nc.scalar.copy(s_win[t][:, S:], zero[:].to_broadcast([P, S]))
+
+        d_scale_picked = sb("d_scale_picked", S, U8, "d_slot")
+        x_scale_picked = sb("x_scale_picked", S, U8, "x_slot")
+        nc.vector.tensor_copy(d_scale_picked[:], d_scale_table[:].indirect(kidx_t[:]))
+        nc.vector.tensor_copy(x_scale_picked[:], x_scale_table[:].indirect(offs_t[:]))
+        planes = sb("planes", 2 * S, U8)
+        nc.vector.tensor_copy(
+            planes[:, 0:S].rearrange("p (t c i) -> p c t i", t=PACK, i=16),
+            d_scale_picked[:].rearrange("p (c i t) -> p c t i", t=PACK, i=16),
+        )
+        nc.vector.tensor_copy(planes[:, S:].bitcast(I32), x_scale_picked[:].bitcast(I32))
+        for r in range(1, 4):
+            nc.scalar.dma_start(planes[r:P:32, :].bitcast(I32), planes[8 * r : P : 32, :].bitcast(I32))
+
+        d_picked = sb("d_picked", S, U32, "x_slot")
+        x_picked = sb("x_picked", S, U32, "d_slot")
+        d_dealt = sb("d_dealt", S, U32)
+        nc.vector.tensor_copy(d_picked[:], d_word_table[:].bitcast(U32).indirect(kidx_t[:]))
+        nc.vector.tensor_copy(x_picked[:], x_word_table[:].bitcast(U32).indirect(offs_t[:]))
+        nc.vector.tensor_copy(
+            d_dealt[:].rearrange("p (t c i) -> p c t i", t=PACK, i=4),
+            d_picked[:].rearrange("p (c i t) -> p c t i", t=PACK, i=4),
+        )
+
+        for t in range(PACK):
+            bank = psum.tile([P, S], F32, name="s_bank%d" % t)
+            cols = slice(t * P, (t + 1) * P)
+            nc.tensor.matmul_mx(
+                out=bank[:],
+                lhsT=d_dealt[:, cols].bitcast(FP8X4),
+                lhsT_scale=planes[:, cols],
+                rhs=x_picked[:].bitcast(FP8X4),
+                rhs_scale=planes[:, S:],
+                start=True,
+                stop=True,
+            )
+            if t == 0:
+                nc.scalar.mul(s_win[t][:, 0:S], bank[:], SIXTEENTH)
+            else:
+                nc.vector.tensor_scalar_mul(s_win[t][:, 0:S], bank[:], SIXTEENTH)
+
+        z2_planes = sb("z2_planes", PACK * S, BF16, "x0")
+        for t in range(PACK):
+            at_n3 = sb("at_n3_%d" % t, S, F32)
+            diff = sb("diff%d" % t, S, F32)
+            nc.scalar.activation(at_n3[:], s_win[t][:].indirect(n3_t[:]), ACT.Copy)
+            if t < 2:
+                nc.vector.tensor_tensor(diff[:], s_win[t][:].indirect(n2_t[:]), at_n3[:], ALU.subtract)
+            else:
+                at_n2 = sb("at_n2_%d" % t, S, F32)
+                nc.scalar.activation(at_n2[:], s_win[t][:].indirect(n2_t[:]), ACT.Copy)
+                nc.vector.tensor_tensor(diff[:], at_n2[:], at_n3[:], ALU.subtract)
+            nc.vector.scalar_tensor_tensor(
+                z2_planes[:, t * S : (t + 1) * S], s_win[t][:, 0:S], gb_t[:, t : t + 1], diff[:], ALU.mult, ALU.mult
+            )
+        z2_codes = sb("z2_codes", S, U32)
+        z2_scale = sb("z2_scale", S, U8)
+        z2_woven = [sb("z2_woven%d" % h, PACK * S // 2, BF16) for h in range(2)]
+        for h in range(2):
+            nc.vector.tensor_copy(
+                z2_woven[h][:].rearrange("p (c i t) -> p c t i", i=4, t=PACK),
+                z2_planes[:].rearrange("p (t h c i) -> p h c t i", t=PACK, h=2, i=4)[:, h],
+            )
+        for h in range(2):
+            cols = slice(h * 256, (h + 1) * 256)
+            nc.vector.quantize_mx(out=z2_codes[:, cols].bitcast(FP8X4), scales=z2_scale[:, cols], in_=z2_woven[h][:])
+
+        def gather_members(h):
+            mb = sb("mb%d" % h, PACK * S, F32)
+            for t in range(PACK):
+                nc.scalar.activation(
+                    mb[:, t * S : (t + 1) * S], s_win[t][:].indirect(n1_t[:, 32 * h : 32 * (h + 1)]), ACT.Copy
+                )
+            return mb
+
+        def first_less_s(h, mb):
+            x = sb("x%d" % h, PACK * 256, F32)
+            for t in range(PACK):
+                nc.vector.tensor_tensor(
+                    x[:, t * 256 : (t + 1) * 256],
+                    mb[:, t * S : (t + 1) * S : 2],
+                    s_win[t][:, h * 256 : (h + 1) * 256],
+                    ALU.subtract,
+                )
+            return x
+
+        def member(mb, u, e):
+            return mb[:].rearrange("p (t u c e) -> p u e t c", t=PACK, u=2, e=2)[:, u, e]
+
+        def step_y(h, u, mb, x):
+            y = sb("y%d_%d" % (h, u), S, F32)
+            nc.vector.scalar_tensor_tensor(
+                y[:].rearrange("p (t c) -> p t c", t=PACK),
+                x[:].rearrange("p (t u c) -> p u t c", t=PACK, u=2)[:, u],
+                0.0,
+                member(mb, u, 1),
+                ALU.min,
+                ALU.add,
+            )
+            return y
+
+        def step_z0(h, u, mb, y):
+            z0 = sb("z0_%d_%d" % (h, u), S, F32, "x1" if (h, u) == (0, 1) else None)
+            nc.vector.tensor_tensor(
+                z0[:].rearrange("p (t c) -> p t c", t=PACK),
+                y[:].rearrange("p (t c) -> p t c", t=PACK),
+                member(mb, u, 0),
+                ALU.min,
+            )
+            return z0
+
+        def step_weave(h, u, z0):
+            zw = sb("zw%d_%d" % (h, u), S, BF16)
+            nc.vector.tensor_tensor(
+                zw[:].rearrange("p (c i t) -> p c t i", i=4, t=PACK),
+                z0[:].rearrange("p (t c i) -> p c t i", i=4, t=PACK),
+                ga_t[:].unsqueeze(1).unsqueeze(3).to_broadcast([P, P // 4, PACK, 4]),
+                ALU.mult,
+            )
+            return zw
+
+        def step_product(m, zw):
+            codes = sb("z_codes%d" % m, P, U32)
+            scale = sb("z_scale%d" % m, P, U8)
+            nc.vector.quantize_mx(out=codes[:].bitcast(FP8X4), scales=scale[:], in_=zw[:])
+            bank = psum.tile([P, S], F32, name="cm_bank%d" % m)
+            nc.tensor.matmul_mx(
+                out=bank[:],
+                lhsT=codes[:].bitcast(FP8X4),
+                lhsT_scale=scale[:],
+                rhs=z2_codes[:].bitcast(FP8X4),
+                rhs_scale=z2_scale[:],
+                start=True,
+                stop=True,
+            )
+            return bank
+
+        def empty_bank(m, bank):
+            cm = sb("cm%d" % m, S, F32)
+            if m == 3:
+                nc.vector.tensor_scalar_mul(cm[:], bank[:], SIXTEENTH)
+            else:
+                nc.scalar.mul(cm[:], bank[:], SIXTEENTH)
+            gate = sb("gate%d" % m, PAIRS, F32)
+            nc.scalar.activation(gate[:], cm[:].indirect(n5_t[:]), ACT.Sigmoid)
+            return cm, gate
+
+        def fold(m, cm, gate):
+            pa = sb("pa%d" % m, PAIRS, F32, ("x1", "y1_1", None, None)[m])
+            if m == 3:
+                nc.vector.tensor_copy(pa[:], cm[:].indirect(n4_t[:]))
+                nc.vector.tensor_tensor(cm[:].indirect(n5_t[:]), pa[:], gate[:], ALU.mult)
+            else:
+                nc.vector.tensor_tensor(pa[:], cm[:].indirect(n4_t[:]), gate[:], ALU.mult)
+                nc.scalar.activation(cm[:].indirect(n5_t[:]), pa[:], ACT.Copy)
+            nc.sync.dma_start(out[m * P : (m + 1) * P, :], cm[:])
+
+        mbs = [gather_members(h) for h in range(2)]
+
+        x = first_less_s(0, mbs[0])
+        ys = [step_y(0, u, mbs[0], x) for u in range(2)]
+        z0s = [step_z0(0, u, mbs[0], ys[u]) for u in range(2)]
+        zws = [step_weave(0, u, z0s[u]) for u in range(2)]
+        banks = [step_product(u, zws[u]) for u in range(2)]
+        early = [empty_bank(u, banks[u]) for u in range(2)]
+
+        x = first_less_s(1, mbs[1])
+        ys = [step_y(1, u, mbs[1], x) for u in range(2)]
+        fold(0, *early[0])
+        z0s = [step_z0(1, u, mbs[1], ys[u]) for u in range(2)]
+        fold(1, *early[1])
+        zws = [step_weave(1, u, z0s[u]) for u in range(2)]
+        banks = [step_product(2 + u, zws[u]) for u in range(2)]
+        late = [empty_bank(2 + u, banks[u]) for u in range(2)]
+        fold(2, *late[0])
+        fold(3, *late[1])

@@ -48,26 +48,37 @@ def tile_picked_simkgpairwindfold_none_p_kernel(
         gb_t = sb("gb_t", PACK, F32)
         kidx_t = load_list("kidx_t", kidx)
         offs_t = load_list("offs_t", offs)
-        n3_t = load_list("n3_t", n3)
-        n2_t = load_list("n2_t", n2)
+        nc.sync.dma_start(ga_t[:], ga.rearrange("(p t) o -> p (t o)", t=PACK))
         nc.sync.dma_start(gb_t[:], gb.rearrange("(p t) o -> p (t o)", t=PACK))
+        n3_t = load_list("n3_t", n3)
         nc.sync.dma_start(d_scale_table[0:P:8, :].bitcast(I32), d_scales[0].bitcast(I32))
         nc.sync.dma_start(x_scale_table[0:P:8, :].bitcast(I32), x_scales[0].bitcast(I32))
         nc.sync.dma_start(d_word_table[:], d_words[0].rearrange("p n t -> p (n t)").bitcast(I32))
         nc.sync.dma_start(x_word_table[:], x_words[0].rearrange("p n t -> p (n t)").bitcast(I32))
+        n2_t = load_list("n2_t", n2)
         n1_t = load_list("n1_t", n1)
-        nc.sync.dma_start(ga_t[:], ga.rearrange("(p t) o -> p (t o)", t=PACK))
         n5_t = load_list("n5_t", n5)
         n4_t = load_list("n4_t", n4)
 
         zero = sb("zero", 1, F32)
         nc.vector.memset(zero[:], 0.0)
+        warm = sb("warm", 1, F32)
+        nc.scalar.activation(warm[:], zero[:], ACT.Sigmoid)
         s_win = [sb("s_win%d" % t, 2 * S, F32) for t in range(PACK)]
-        for t in range(PACK):
-            nc.scalar.copy(s_win[t][:, S:], zero[:].to_broadcast([P, S]))
+        w_win = [sb("w_win%d" % t, 2 * S, F32) for t in range(PACK)]
+        for win in s_win + w_win:
+            nc.scalar.copy(win[:, S:], zero[:].to_broadcast([P, S]))
 
-        d_scale_picked = sb("d_scale_picked", S, U8, "d_slot")
-        x_scale_picked = sb("x_scale_picked", S, U8, "x_slot")
+        sign = sb("sign", PACK, F32)
+        ga_abs = sb("ga_abs", PACK, F32)
+        gb_signed = sb("gb_signed", PACK, F32)
+        nc.gpsimd.tensor_scalar(sign[:], ga_t[:], 0.0, 2.0, ALU.is_ge, ALU.mult)
+        nc.gpsimd.tensor_scalar(sign[:], sign[:], -1.0, 1.0, ALU.add, ALU.mult)
+        nc.gpsimd.tensor_tensor(ga_abs[:], ga_t[:], sign[:], ALU.mult)
+        nc.gpsimd.tensor_tensor(gb_signed[:], gb_t[:], sign[:], ALU.mult)
+
+        d_scale_picked = sb("d_scale_picked", S, U8)
+        x_scale_picked = sb("x_scale_picked", S, U8)
         nc.vector.tensor_copy(d_scale_picked[:], d_scale_table[:].indirect(kidx_t[:]))
         nc.vector.tensor_copy(x_scale_picked[:], x_scale_table[:].indirect(offs_t[:]))
         planes = sb("planes", 2 * S, U8)
@@ -77,10 +88,10 @@ def tile_picked_simkgpairwindfold_none_p_kernel(
         )
         nc.vector.tensor_copy(planes[:, S:].bitcast(I32), x_scale_picked[:].bitcast(I32))
         for r in range(1, 4):
-            nc.scalar.dma_start(planes[r:P:32, :].bitcast(I32), planes[8 * r : P : 32, :].bitcast(I32))
+            nc.sync.dma_start(planes[r:P:32, :].bitcast(I32), planes[8 * r : P : 32, :].bitcast(I32))
 
-        d_picked = sb("d_picked", S, U32, "x_slot")
-        x_picked = sb("x_picked", S, U32, "d_slot")
+        d_picked = sb("d_picked", S, U32)
+        x_picked = sb("x_picked", S, U32)
         d_dealt = sb("d_dealt", S, U32)
         nc.vector.tensor_copy(d_picked[:], d_word_table[:].bitcast(U32).indirect(kidx_t[:]))
         nc.vector.tensor_copy(x_picked[:], x_word_table[:].bitcast(U32).indirect(offs_t[:]))
@@ -89,6 +100,7 @@ def tile_picked_simkgpairwindfold_none_p_kernel(
             d_picked[:].rearrange("p (c i t) -> p c t i", t=PACK, i=4),
         )
 
+        s_banks = []
         for t in range(PACK):
             bank = psum.tile([P, S], F32, name="s_bank%d" % t)
             cols = slice(t * P, (t + 1) * P)
@@ -101,24 +113,21 @@ def tile_picked_simkgpairwindfold_none_p_kernel(
                 start=True,
                 stop=True,
             )
-            if t == 0:
-                nc.scalar.mul(s_win[t][:, 0:S], bank[:], SIXTEENTH)
-            else:
-                nc.vector.tensor_scalar_mul(s_win[t][:, 0:S], bank[:], SIXTEENTH)
+            s_banks.append(bank)
 
         z2_planes = sb("z2_planes", PACK * S, BF16, "x0")
         for t in range(PACK):
+            if t == 1:
+                nc.vector.tensor_scalar_mul(s_win[t][:, 0:S], s_banks[t][:], SIXTEENTH)
+            else:
+                nc.scalar.mul(s_win[t][:, 0:S], s_banks[t][:], SIXTEENTH)
+            nc.vector.tensor_scalar_mul(w_win[t][:, 0:S], s_win[t][:, 0:S], ga_abs[:, t : t + 1])
             at_n3 = sb("at_n3_%d" % t, S, F32)
             diff = sb("diff%d" % t, S, F32)
             nc.scalar.activation(at_n3[:], s_win[t][:].indirect(n3_t[:]), ACT.Copy)
-            if t < 2:
-                nc.vector.tensor_tensor(diff[:], s_win[t][:].indirect(n2_t[:]), at_n3[:], ALU.subtract)
-            else:
-                at_n2 = sb("at_n2_%d" % t, S, F32)
-                nc.scalar.activation(at_n2[:], s_win[t][:].indirect(n2_t[:]), ACT.Copy)
-                nc.vector.tensor_tensor(diff[:], at_n2[:], at_n3[:], ALU.subtract)
+            nc.vector.tensor_tensor(diff[:], s_win[t][:].indirect(n2_t[:]), at_n3[:], ALU.subtract)
             nc.vector.scalar_tensor_tensor(
-                z2_planes[:, t * S : (t + 1) * S], s_win[t][:, 0:S], gb_t[:, t : t + 1], diff[:], ALU.mult, ALU.mult
+                z2_planes[:, t * S : (t + 1) * S], s_win[t][:, 0:S], gb_signed[:, t : t + 1], diff[:], ALU.mult, ALU.mult
             )
         z2_codes = sb("z2_codes", S, U32)
         z2_scale = sb("z2_scale", S, U8)
@@ -133,10 +142,10 @@ def tile_picked_simkgpairwindfold_none_p_kernel(
             nc.vector.quantize_mx(out=z2_codes[:, cols].bitcast(FP8X4), scales=z2_scale[:, cols], in_=z2_woven[h][:])
 
         def gather_members(h):
-            mb = sb("mb%d" % h, PACK * S, F32)
+            mb = sb("mb%d" % h, PACK * S, F32, "at_n3_3" if h == 1 else None)
             for t in range(PACK):
                 nc.scalar.activation(
-                    mb[:, t * S : (t + 1) * S], s_win[t][:].indirect(n1_t[:, 32 * h : 32 * (h + 1)]), ACT.Copy
+                    mb[:, t * S : (t + 1) * S], w_win[t][:].indirect(n1_t[:, 32 * h : 32 * (h + 1)]), ACT.Copy
                 )
             return mb
 
@@ -146,7 +155,7 @@ def tile_picked_simkgpairwindfold_none_p_kernel(
                 nc.vector.tensor_tensor(
                     x[:, t * 256 : (t + 1) * 256],
                     mb[:, t * S : (t + 1) * S : 2],
-                    s_win[t][:, h * 256 : (h + 1) * 256],
+                    w_win[t][:, h * 256 : (h + 1) * 256],
                     ALU.subtract,
                 )
             return x
@@ -155,7 +164,7 @@ def tile_picked_simkgpairwindfold_none_p_kernel(
             return mb[:].rearrange("p (t u c e) -> p u e t c", t=PACK, u=2, e=2)[:, u, e]
 
         def step_y(h, u, mb, x):
-            y = sb("y%d_%d" % (h, u), S, F32)
+            y = sb("y%d_%d" % (h, u), S, F32, "x1" if (h, u) == (0, 1) else None)
             nc.vector.scalar_tensor_tensor(
                 y[:].rearrange("p (t c) -> p t c", t=PACK),
                 x[:].rearrange("p (t u c) -> p u t c", t=PACK, u=2)[:, u],
@@ -166,23 +175,13 @@ def tile_picked_simkgpairwindfold_none_p_kernel(
             )
             return y
 
-        def step_z0(h, u, mb, y):
-            z0 = sb("z0_%d_%d" % (h, u), S, F32, "x1" if (h, u) == (0, 1) else None)
-            nc.vector.tensor_tensor(
-                z0[:].rearrange("p (t c) -> p t c", t=PACK),
-                y[:].rearrange("p (t c) -> p t c", t=PACK),
-                member(mb, u, 0),
-                ALU.min,
-            )
-            return z0
-
-        def step_weave(h, u, z0):
+        def step_weave(h, u, mb, y):
             zw = sb("zw%d_%d" % (h, u), S, BF16)
             nc.vector.tensor_tensor(
                 zw[:].rearrange("p (c i t) -> p c t i", i=4, t=PACK),
-                z0[:].rearrange("p (t c i) -> p c t i", i=4, t=PACK),
-                ga_t[:].unsqueeze(1).unsqueeze(3).to_broadcast([P, P // 4, PACK, 4]),
-                ALU.mult,
+                y[:].rearrange("p (t c i) -> p c t i", i=4, t=PACK),
+                mb[:].rearrange("p (t u c i e) -> p u e c t i", t=PACK, u=2, i=4, e=2)[:, u, 0],
+                ALU.min,
             )
             return zw
 
@@ -208,36 +207,47 @@ def tile_picked_simkgpairwindfold_none_p_kernel(
                 nc.vector.tensor_scalar_mul(cm[:], bank[:], SIXTEENTH)
             else:
                 nc.scalar.mul(cm[:], bank[:], SIXTEENTH)
+            return cm
+
+        def gate_of(m, cm):
             gate = sb("gate%d" % m, PAIRS, F32)
             nc.scalar.activation(gate[:], cm[:].indirect(n5_t[:]), ACT.Sigmoid)
-            return cm, gate
+            return gate
 
-        def fold(m, cm, gate):
-            pa = sb("pa%d" % m, PAIRS, F32, ("x1", "y1_1", None, None)[m])
-            if m == 3:
-                nc.vector.tensor_copy(pa[:], cm[:].indirect(n4_t[:]))
-                nc.vector.tensor_tensor(cm[:].indirect(n5_t[:]), pa[:], gate[:], ALU.mult)
-            else:
-                nc.vector.tensor_tensor(pa[:], cm[:].indirect(n4_t[:]), gate[:], ALU.mult)
-                nc.scalar.activation(cm[:].indirect(n5_t[:]), pa[:], ACT.Copy)
+        def store(m, cm):
             nc.sync.dma_start(out[m * P : (m + 1) * P, :], cm[:])
 
         mbs = [gather_members(h) for h in range(2)]
 
         x = first_less_s(0, mbs[0])
         ys = [step_y(0, u, mbs[0], x) for u in range(2)]
-        z0s = [step_z0(0, u, mbs[0], ys[u]) for u in range(2)]
-        zws = [step_weave(0, u, z0s[u]) for u in range(2)]
+        zws = [step_weave(0, u, mbs[0], ys[u]) for u in range(2)]
         banks = [step_product(u, zws[u]) for u in range(2)]
-        early = [empty_bank(u, banks[u]) for u in range(2)]
+        cms, gates = [], []
+        for u in range(2):
+            cms.append(empty_bank(u, banks[u]))
+            gates.append(gate_of(u, cms[u]))
 
         x = first_less_s(1, mbs[1])
         ys = [step_y(1, u, mbs[1], x) for u in range(2)]
-        fold(0, *early[0])
-        z0s = [step_z0(1, u, mbs[1], ys[u]) for u in range(2)]
-        fold(1, *early[1])
-        zws = [step_weave(1, u, z0s[u]) for u in range(2)]
-        banks = [step_product(2 + u, zws[u]) for u in range(2)]
-        late = [empty_bank(2 + u, banks[u]) for u in range(2)]
-        fold(2, *late[0])
-        fold(3, *late[1])
+        zws = [step_weave(1, u, mbs[1], ys[u]) for u in range(2)]
+        ra0 = sb("ra0", PAIRS, F32, "y1_0")
+        pa1 = sb("pa1", PAIRS, F32, "y1_1")
+        banks = [step_product(2, zws[0])]
+        nc.vector.tensor_tensor(ra0[:], cms[0][:].indirect(n4_t[:]), gates[0][:], ALU.mult)
+        banks.append(step_product(3, zws[1]))
+        nc.scalar.activation(pa1[:], cms[1][:].indirect(n4_t[:]), ACT.Copy)
+        nc.scalar.activation(cms[0][:].indirect(n5_t[:]), ra0[:], ACT.Copy)
+        nc.vector.tensor_tensor(cms[1][:].indirect(n5_t[:]), pa1[:], gates[1][:], ALU.mult)
+        for u in range(2):
+            store(u, cms[u])
+        cms = [empty_bank(2 + u, banks[u]) for u in range(2)]
+        gates = [gate_of(2 + u, cms[u]) for u in range(2)]
+        pa3 = sb("pa3", PAIRS, F32)
+        ra2 = sb("ra2", PAIRS, F32)
+        nc.vector.tensor_copy(pa3[:], cms[1][:].indirect(n4_t[:]))
+        nc.vector.tensor_tensor(ra2[:], cms[0][:].indirect(n4_t[:]), gates[0][:], ALU.mult)
+        nc.scalar.activation(cms[0][:].indirect(n5_t[:]), ra2[:], ACT.Copy)
+        nc.vector.tensor_tensor(cms[1][:].indirect(n5_t[:]), pa3[:], gates[1][:], ALU.mult)
+        for u in range(2):
+            store(2 + u, cms[u])

@@ -13,10 +13,13 @@ ALU = mybir.AluOpType
 ACT = mybir.ActivationFunctionType
 
 P = 128
-PACK = 4
+PLANES = 4
 TABLE = 2048
 S = 512
+HALF = S // 2
 PAIRS = 256
+LINE = 16
+WEAVE = 4
 SIXTEENTH = 0.0625
 FLOPS = 2 * 2 * 512 * 512 * 512
 
@@ -29,166 +32,177 @@ def tile_picked_simkgpairwindfold_none_p_kernel(
         keep = ctx.enter_context(tc.tile_pool(name="keep", bufs=1))
         psum = ctx.enter_context(tc.psum_pool(name="psum", bufs=1))
 
-        def sb(name, cols, dtype, tag=None):
-            return keep.tile([P, cols], dtype, name=name, tag=tag or name, align_bytes=64)
+        def sbuf(name, cols, dtype, slot=None):
+            return keep.tile([P, cols], dtype, name=name, tag=slot or name, align_bytes=64)
 
         def load_list(name, src):
-            t = keep.tile(list(src.shape), U16, name=name)
-            nc.sync.dma_start(t[:], src)
-            return t
+            offsets = keep.tile(list(src.shape), U16, name=name)
+            nc.sync.dma_start(offsets[:], src)
+            return offsets
 
-        d_scale_table = sb("d_scale_table", TABLE, U8)
-        x_scale_table = sb("x_scale_table", TABLE, U8)
+        d_scale_table = sbuf("d_scale_table", TABLE, U8)
+        x_scale_table = sbuf("x_scale_table", TABLE, U8)
         for table in (d_scale_table, x_scale_table):
             nc.vector.memset(table[:, 0 : TABLE // 2].bitcast(I32), 0)
             nc.gpsimd.memset(table[:, TABLE // 2 :].bitcast(I32), 0)
-        d_word_table = sb("d_word_table", TABLE, I32)
-        x_word_table = sb("x_word_table", TABLE, I32)
-        ga_t = sb("ga_t", PACK, F32)
-        gb_t = sb("gb_t", PACK, F32)
-        kidx_t = load_list("kidx_t", kidx)
-        offs_t = load_list("offs_t", offs)
-        nc.sync.dma_start(ga_t[:], ga.rearrange("(p t) o -> p (t o)", t=PACK))
-        nc.sync.dma_start(gb_t[:], gb.rearrange("(p t) o -> p (t o)", t=PACK))
-        n3_t = load_list("n3_t", n3)
+        d_word_table = sbuf("d_word_table", TABLE, I32)
+        x_word_table = sbuf("x_word_table", TABLE, I32)
+        ga_keys = sbuf("ga_keys", PLANES, F32)
+        gb_keys = sbuf("gb_keys", PLANES, F32)
+        kidx_list = load_list("kidx_list", kidx)
+        offs_list = load_list("offs_list", offs)
+        nc.sync.dma_start(ga_keys[:], ga.rearrange("(p t) o -> p (t o)", t=PLANES))
+        nc.sync.dma_start(gb_keys[:], gb.rearrange("(p t) o -> p (t o)", t=PLANES))
+        n3_list = load_list("n3_list", n3)
         nc.sync.dma_start(d_scale_table[0:P:8, :].bitcast(I32), d_scales[0].bitcast(I32))
         nc.sync.dma_start(x_scale_table[0:P:8, :].bitcast(I32), x_scales[0].bitcast(I32))
         nc.sync.dma_start(d_word_table[:], d_words[0].rearrange("p n t -> p (n t)").bitcast(I32))
         nc.sync.dma_start(x_word_table[:], x_words[0].rearrange("p n t -> p (n t)").bitcast(I32))
-        n2_t = load_list("n2_t", n2)
-        n1_t = load_list("n1_t", n1)
-        n5_t = load_list("n5_t", n5)
-        n4_t = load_list("n4_t", n4)
+        n2_list = load_list("n2_list", n2)
+        n1_list = load_list("n1_list", n1)
+        n5_list = load_list("n5_list", n5)
+        n4_list = load_list("n4_list", n4)
 
-        zero = sb("zero", 1, F32)
+        zero = sbuf("zero", 1, F32)
         nc.vector.memset(zero[:], 0.0)
-        warm = sb("warm", 1, F32)
-        nc.scalar.activation(warm[:], zero[:], ACT.Sigmoid)
-        s_win = [sb("s_win%d" % t, 2 * S, F32) for t in range(PACK)]
-        w_win = [sb("w_win%d" % t, 2 * S, F32) for t in range(PACK)]
+        warm_up = sbuf("warm_up", 1, F32)
+        nc.scalar.activation(warm_up[:], zero[:], ACT.Sigmoid)
+        s_win = [sbuf("s_win%d" % t, 2 * S, F32) for t in range(PLANES)]
+        w_win = [sbuf("w_win%d" % t, 2 * S, F32) for t in range(PLANES)]
         for win in s_win + w_win:
             nc.scalar.copy(win[:, S:], zero[:].to_broadcast([P, S]))
 
-        sign = sb("sign", PACK, F32)
-        ga_abs = sb("ga_abs", PACK, F32)
-        gb_signed = sb("gb_signed", PACK, F32)
-        nc.gpsimd.tensor_scalar(sign[:], ga_t[:], 0.0, 2.0, ALU.is_ge, ALU.mult)
+        sign = sbuf("sign", PLANES, F32)
+        ga_abs = sbuf("ga_abs", PLANES, F32)
+        gb_signed = sbuf("gb_signed", PLANES, F32)
+        nc.gpsimd.tensor_scalar(sign[:], ga_keys[:], 0.0, 2.0, ALU.is_ge, ALU.mult)
         nc.gpsimd.tensor_scalar(sign[:], sign[:], -1.0, 1.0, ALU.add, ALU.mult)
-        nc.gpsimd.tensor_tensor(ga_abs[:], ga_t[:], sign[:], ALU.mult)
-        nc.gpsimd.tensor_tensor(gb_signed[:], gb_t[:], sign[:], ALU.mult)
+        nc.gpsimd.tensor_tensor(ga_abs[:], ga_keys[:], sign[:], ALU.mult)
+        nc.gpsimd.tensor_tensor(gb_signed[:], gb_keys[:], sign[:], ALU.mult)
 
-        d_scale_picked = sb("d_scale_picked", S, U8)
-        x_scale_picked = sb("x_scale_picked", S, U8)
-        nc.vector.tensor_copy(d_scale_picked[:], d_scale_table[:].indirect(kidx_t[:]))
-        nc.vector.tensor_copy(x_scale_picked[:], x_scale_table[:].indirect(offs_t[:]))
-        planes = sb("planes", 2 * S, U8)
+        d_scale_picked = sbuf("d_scale_picked", S, U8)
+        x_scale_picked = sbuf("x_scale_picked", S, U8)
+        nc.vector.tensor_copy(d_scale_picked[:], d_scale_table[:].indirect(kidx_list[:]))
+        nc.vector.tensor_copy(x_scale_picked[:], x_scale_table[:].indirect(offs_list[:]))
+        scale_rows = sbuf("scale_rows", 2 * S, U8)
         nc.vector.tensor_copy(
-            planes[:, 0:S].rearrange("p (t c i) -> p c t i", t=PACK, i=16),
-            d_scale_picked[:].rearrange("p (c i t) -> p c t i", t=PACK, i=16),
+            scale_rows[:, 0:S].rearrange("p (t c i) -> p c t i", t=PLANES, i=LINE),
+            d_scale_picked[:].rearrange("p (c i t) -> p c t i", t=PLANES, i=LINE),
         )
-        nc.vector.tensor_copy(planes[:, S:].bitcast(I32), x_scale_picked[:].bitcast(I32))
+        nc.vector.tensor_copy(scale_rows[:, S:].bitcast(I32), x_scale_picked[:].bitcast(I32))
         for r in range(1, 4):
-            nc.sync.dma_start(planes[r:P:32, :].bitcast(I32), planes[8 * r : P : 32, :].bitcast(I32))
+            nc.sync.dma_start(scale_rows[r:P:32, :].bitcast(I32), scale_rows[8 * r : P : 32, :].bitcast(I32))
 
-        d_picked = sb("d_picked", S, U32)
-        x_picked = sb("x_picked", S, U32)
-        d_dealt = sb("d_dealt", S, U32)
-        nc.vector.tensor_copy(d_picked[:], d_word_table[:].bitcast(U32).indirect(kidx_t[:]))
-        nc.vector.tensor_copy(x_picked[:], x_word_table[:].bitcast(U32).indirect(offs_t[:]))
+        d_picked = sbuf("d_picked", S, U32)
+        x_picked = sbuf("x_picked", S, U32)
+        d_dealt = sbuf("d_dealt", S, U32)
+        nc.vector.tensor_copy(d_picked[:], d_word_table[:].bitcast(U32).indirect(kidx_list[:]))
+        nc.vector.tensor_copy(x_picked[:], x_word_table[:].bitcast(U32).indirect(offs_list[:]))
         nc.vector.tensor_copy(
-            d_dealt[:].rearrange("p (t c i) -> p c t i", t=PACK, i=4),
-            d_picked[:].rearrange("p (c i t) -> p c t i", t=PACK, i=4),
+            d_dealt[:].rearrange("p (t c i) -> p c t i", t=PLANES, i=LINE // 4),
+            d_picked[:].rearrange("p (c i t) -> p c t i", t=PLANES, i=LINE // 4),
         )
 
-        s_banks = []
-        for t in range(PACK):
-            bank = psum.tile([P, S], F32, name="s_bank%d" % t)
-            cols = slice(t * P, (t + 1) * P)
+        def first_product(bank, t, tokens):
+            keys = slice(t * P, (t + 1) * P)
             nc.tensor.matmul_mx(
-                out=bank[:],
-                lhsT=d_dealt[:, cols].bitcast(FP8X4),
-                lhsT_scale=planes[:, cols],
-                rhs=x_picked[:].bitcast(FP8X4),
-                rhs_scale=planes[:, S:],
+                out=bank,
+                lhsT=d_dealt[:, keys].bitcast(FP8X4),
+                lhsT_scale=scale_rows[:, keys],
+                rhs=x_picked[:, tokens].bitcast(FP8X4),
+                rhs_scale=scale_rows[:, S + tokens.start : S + tokens.stop],
                 start=True,
                 stop=True,
             )
-            s_banks.append(bank)
 
-        z2_planes = sb("z2_planes", PACK * S, BF16, "x0")
-        for t in range(PACK):
-            if t == 1:
-                nc.vector.tensor_scalar_mul(s_win[t][:, 0:S], s_banks[t][:], SIXTEENTH)
+        left, right, every = slice(0, HALF), slice(HALF, S), slice(0, S)
+        s_banks = [psum.tile([P, S], F32, name="s_bank%d" % t) for t in range(PLANES)]
+        right_bank = psum.tile([P, S], F32, name="cm_bank3")
+        first_product(s_banks[0][:, left], 0, left)
+        first_product(right_bank[:, left], 0, right)
+        for t in range(1, PLANES):
+            first_product(s_banks[t][:], t, every)
+        nc.scalar.mul(s_win[0][:, left], s_banks[0][:, left], SIXTEENTH)
+        nc.vector.tensor_scalar_mul(s_win[0][:, right], right_bank[:, left], SIXTEENTH)
+        for t in (1, 2):
+            nc.vector.tensor_scalar_mul(s_win[t][:, every], s_banks[t][:], SIXTEENTH)
+
+        last = PLANES - 1
+        z2_planes = sbuf("z2_planes", PLANES * S, BF16, "first_less_s0")
+        for t in range(PLANES):
+            if t == last:
+                nc.scalar.mul(s_win[t][:, every], s_banks[t][:], SIXTEENTH)
             else:
-                nc.scalar.mul(s_win[t][:, 0:S], s_banks[t][:], SIXTEENTH)
-            nc.vector.tensor_scalar_mul(w_win[t][:, 0:S], s_win[t][:, 0:S], ga_abs[:, t : t + 1])
-            at_n3 = sb("at_n3_%d" % t, S, F32)
-            diff = sb("diff%d" % t, S, F32)
-            nc.scalar.activation(at_n3[:], s_win[t][:].indirect(n3_t[:]), ACT.Copy)
-            nc.vector.tensor_tensor(diff[:], s_win[t][:].indirect(n2_t[:]), at_n3[:], ALU.subtract)
+                nc.vector.tensor_scalar_mul(w_win[t][:, every], s_win[t][:, every], ga_abs[:, t : t + 1])
+            at_n3 = sbuf("at_n3_%d" % t, S, F32)
+            diff = sbuf("diff%d" % t, S, F32)
+            nc.scalar.activation(at_n3[:], s_win[t][:].indirect(n3_list[:]), ACT.Copy)
+            if t == last:
+                nc.scalar.activation(w_win[t][:, every], s_win[t][:, every], ACT.Copy, scale=ga_abs[:, t : t + 1])
+            nc.vector.tensor_tensor(diff[:], s_win[t][:].indirect(n2_list[:]), at_n3[:], ALU.subtract)
             nc.vector.scalar_tensor_tensor(
-                z2_planes[:, t * S : (t + 1) * S], s_win[t][:, 0:S], gb_signed[:, t : t + 1], diff[:], ALU.mult, ALU.mult
+                z2_planes[:, t * S : (t + 1) * S],
+                s_win[t][:, every],
+                gb_signed[:, t : t + 1],
+                diff[:],
+                ALU.mult,
+                ALU.mult,
             )
-        z2_codes = sb("z2_codes", S, U32)
-        z2_scale = sb("z2_scale", S, U8)
-        z2_woven = [sb("z2_woven%d" % h, PACK * S // 2, BF16) for h in range(2)]
+        z2_codes = sbuf("z2_codes", S, U32)
+        z2_scale = sbuf("z2_scale", S, U8)
+        z2_woven = [sbuf("z2_woven%d" % h, PLANES * HALF, BF16) for h in range(2)]
         for h in range(2):
             nc.vector.tensor_copy(
-                z2_woven[h][:].rearrange("p (c i t) -> p c t i", i=4, t=PACK),
-                z2_planes[:].rearrange("p (t h c i) -> p h c t i", t=PACK, h=2, i=4)[:, h],
+                z2_woven[h][:].rearrange("p (c i t) -> p c t i", i=WEAVE, t=PLANES),
+                z2_planes[:].rearrange("p (t h c i) -> p h c t i", t=PLANES, h=2, i=WEAVE)[:, h],
             )
-        for h in range(2):
-            cols = slice(h * 256, (h + 1) * 256)
+        for h, cols in enumerate((left, right)):
             nc.vector.quantize_mx(out=z2_codes[:, cols].bitcast(FP8X4), scales=z2_scale[:, cols], in_=z2_woven[h][:])
 
-        def gather_members(h):
-            mb = sb("mb%d" % h, PACK * S, F32, "at_n3_3" if h == 1 else None)
-            for t in range(PACK):
-                nc.scalar.activation(
-                    mb[:, t * S : (t + 1) * S], w_win[t][:].indirect(n1_t[:, 32 * h : 32 * (h + 1)]), ACT.Copy
-                )
-            return mb
+        def gather_members(h, slot):
+            members = sbuf("members%d" % h, PLANES * S, F32, slot)
+            entries = n1_list[:, h * S // 16 : (h + 1) * S // 16]
+            for t in range(PLANES):
+                nc.scalar.activation(members[:, t * S : (t + 1) * S], w_win[t][:].indirect(entries), ACT.Copy)
+            return members
 
-        def first_less_s(h, mb):
-            x = sb("x%d" % h, PACK * 256, F32)
-            for t in range(PACK):
+        def first_less_s(h, members):
+            less = sbuf("first_less_s%d" % h, PLANES * HALF, F32)
+            for t in range(PLANES):
                 nc.vector.tensor_tensor(
-                    x[:, t * 256 : (t + 1) * 256],
-                    mb[:, t * S : (t + 1) * S : 2],
-                    w_win[t][:, h * 256 : (h + 1) * 256],
+                    less[:, t * HALF : (t + 1) * HALF],
+                    members[:, t * S : (t + 1) * S : 2],
+                    w_win[t][:, h * HALF : (h + 1) * HALF],
                     ALU.subtract,
                 )
-            return x
+            return less
 
-        def member(mb, u, e):
-            return mb[:].rearrange("p (t u c e) -> p u e t c", t=PACK, u=2, e=2)[:, u, e]
-
-        def step_y(h, u, mb, x):
-            y = sb("y%d_%d" % (h, u), S, F32, "x1" if (h, u) == (0, 1) else None)
+        def plus_second(h, u, members, less, slot):
+            summed = sbuf("summed%d_%d" % (h, u), S, F32, slot)
             nc.vector.scalar_tensor_tensor(
-                y[:].rearrange("p (t c) -> p t c", t=PACK),
-                x[:].rearrange("p (t u c) -> p u t c", t=PACK, u=2)[:, u],
+                summed[:].rearrange("p (t c) -> p t c", t=PLANES),
+                less[:].rearrange("p (t u c) -> p u t c", t=PLANES, u=2)[:, u],
                 0.0,
-                member(mb, u, 1),
+                members[:].rearrange("p (t u c e) -> p u e t c", t=PLANES, u=2, e=2)[:, u, 1],
                 ALU.min,
                 ALU.add,
             )
-            return y
+            return summed
 
-        def step_weave(h, u, mb, y):
-            zw = sb("zw%d_%d" % (h, u), S, BF16)
+        def weave_z(h, u, members, summed):
+            woven = sbuf("z_woven%d_%d" % (h, u), S, BF16)
             nc.vector.tensor_tensor(
-                zw[:].rearrange("p (c i t) -> p c t i", i=4, t=PACK),
-                y[:].rearrange("p (t c i) -> p c t i", i=4, t=PACK),
-                mb[:].rearrange("p (t u c i e) -> p u e c t i", t=PACK, u=2, i=4, e=2)[:, u, 0],
+                woven[:].rearrange("p (c i t) -> p c t i", i=WEAVE, t=PLANES),
+                summed[:].rearrange("p (t c i) -> p c t i", i=WEAVE, t=PLANES),
+                members[:].rearrange("p (t u c i e) -> p u e c t i", t=PLANES, u=2, i=WEAVE, e=2)[:, u, 0],
                 ALU.min,
             )
-            return zw
+            return woven
 
-        def step_product(m, zw):
-            codes = sb("z_codes%d" % m, P, U32)
-            scale = sb("z_scale%d" % m, P, U8)
-            nc.vector.quantize_mx(out=codes[:].bitcast(FP8X4), scales=scale[:], in_=zw[:])
+        def second_product(m, woven):
+            codes = sbuf("z_codes%d" % m, P, U32)
+            scale = sbuf("z_scale%d" % m, P, U8)
+            nc.vector.quantize_mx(out=codes[:].bitcast(FP8X4), scales=scale[:], in_=woven[:])
             bank = psum.tile([P, S], F32, name="cm_bank%d" % m)
             nc.tensor.matmul_mx(
                 out=bank[:],
@@ -201,53 +215,53 @@ def tile_picked_simkgpairwindfold_none_p_kernel(
             )
             return bank
 
-        def empty_bank(m, bank):
-            cm = sb("cm%d" % m, S, F32)
-            if m == 3:
-                nc.vector.tensor_scalar_mul(cm[:], bank[:], SIXTEENTH)
-            else:
-                nc.scalar.mul(cm[:], bank[:], SIXTEENTH)
+        def empty_bank(m, bank, scale_by):
+            cm = sbuf("cm%d" % m, S, F32)
+            scale_by(cm[:], bank[:], SIXTEENTH)
             return cm
 
         def gate_of(m, cm):
-            gate = sb("gate%d" % m, PAIRS, F32)
-            nc.scalar.activation(gate[:], cm[:].indirect(n5_t[:]), ACT.Sigmoid)
+            gate = sbuf("gate%d" % m, PAIRS, F32)
+            nc.scalar.activation(gate[:], cm[:].indirect(n5_list[:]), ACT.Sigmoid)
             return gate
 
         def store(m, cm):
             nc.sync.dma_start(out[m * P : (m + 1) * P, :], cm[:])
 
-        mbs = [gather_members(h) for h in range(2)]
+        members = [gather_members(0, None), gather_members(1, "at_n3_%d" % last)]
 
-        x = first_less_s(0, mbs[0])
-        ys = [step_y(0, u, mbs[0], x) for u in range(2)]
-        zws = [step_weave(0, u, mbs[0], ys[u]) for u in range(2)]
-        banks = [step_product(u, zws[u]) for u in range(2)]
+        less = first_less_s(0, members[0])
+        summed = [plus_second(0, 0, members[0], less, None), plus_second(0, 1, members[0], less, "first_less_s1")]
+        woven = [weave_z(0, u, members[0], summed[u]) for u in range(2)]
+        banks = [second_product(u, woven[u]) for u in range(2)]
         cms, gates = [], []
-        for u in range(2):
-            cms.append(empty_bank(u, banks[u]))
-            gates.append(gate_of(u, cms[u]))
+        for m in (0, 1):
+            cms.append(empty_bank(m, banks[m], nc.scalar.mul))
+            gates.append(gate_of(m, cms[m]))
 
-        x = first_less_s(1, mbs[1])
-        ys = [step_y(1, u, mbs[1], x) for u in range(2)]
-        zws = [step_weave(1, u, mbs[1], ys[u]) for u in range(2)]
-        ra0 = sb("ra0", PAIRS, F32, "y1_0")
-        pa1 = sb("pa1", PAIRS, F32, "y1_1")
-        banks = [step_product(2, zws[0])]
-        nc.vector.tensor_tensor(ra0[:], cms[0][:].indirect(n4_t[:]), gates[0][:], ALU.mult)
-        banks.append(step_product(3, zws[1]))
-        nc.scalar.activation(pa1[:], cms[1][:].indirect(n4_t[:]), ACT.Copy)
-        nc.scalar.activation(cms[0][:].indirect(n5_t[:]), ra0[:], ACT.Copy)
-        nc.vector.tensor_tensor(cms[1][:].indirect(n5_t[:]), pa1[:], gates[1][:], ALU.mult)
-        for u in range(2):
-            store(u, cms[u])
-        cms = [empty_bank(2 + u, banks[u]) for u in range(2)]
-        gates = [gate_of(2 + u, cms[u]) for u in range(2)]
-        pa3 = sb("pa3", PAIRS, F32)
-        ra2 = sb("ra2", PAIRS, F32)
-        nc.vector.tensor_copy(pa3[:], cms[1][:].indirect(n4_t[:]))
-        nc.vector.tensor_tensor(ra2[:], cms[0][:].indirect(n4_t[:]), gates[0][:], ALU.mult)
-        nc.scalar.activation(cms[0][:].indirect(n5_t[:]), ra2[:], ACT.Copy)
-        nc.vector.tensor_tensor(cms[1][:].indirect(n5_t[:]), pa3[:], gates[1][:], ALU.mult)
-        for u in range(2):
-            store(2 + u, cms[u])
+        less = first_less_s(1, members[1])
+        summed = [plus_second(1, u, members[1], less, None) for u in range(2)]
+        woven = [weave_z(1, u, members[1], summed[u]) for u in range(2)]
+
+        ra0 = sbuf("ra0", PAIRS, F32, "summed1_0")
+        pa1 = sbuf("pa1", PAIRS, F32, "summed1_1")
+        banks.append(second_product(2, woven[0]))
+        nc.vector.tensor_tensor(ra0[:], cms[0][:].indirect(n4_list[:]), gates[0][:], ALU.mult)
+        banks.append(second_product(3, woven[1]))
+        nc.scalar.activation(pa1[:], cms[1][:].indirect(n4_list[:]), ACT.Copy)
+        nc.scalar.activation(cms[0][:].indirect(n5_list[:]), ra0[:], ACT.Copy)
+        nc.vector.tensor_tensor(cms[1][:].indirect(n5_list[:]), pa1[:], gates[1][:], ALU.mult)
+        for m in (0, 1):
+            store(m, cms[m])
+
+        cms.append(empty_bank(2, banks[2], nc.scalar.mul))
+        cms.append(empty_bank(3, banks[3], nc.vector.tensor_scalar_mul))
+        gates.extend([gate_of(m, cms[m]) for m in (2, 3)])
+        pa3 = sbuf("pa3", PAIRS, F32)
+        ra2 = sbuf("ra2", PAIRS, F32)
+        nc.vector.tensor_copy(pa3[:], cms[3][:].indirect(n4_list[:]))
+        nc.vector.tensor_tensor(ra2[:], cms[2][:].indirect(n4_list[:]), gates[2][:], ALU.mult)
+        nc.scalar.activation(cms[2][:].indirect(n5_list[:]), ra2[:], ACT.Copy)
+        nc.vector.tensor_tensor(cms[3][:].indirect(n5_list[:]), pa3[:], gates[3][:], ALU.mult)
+        for m in (2, 3):
+            store(m, cms[m])

@@ -20,6 +20,7 @@ HALF = S // 2
 PAIRS = 256
 LINE = 16
 WEAVE = 4
+WEAVE_Z = 2
 SIXTEENTH = 0.0625
 FLOPS = 2 * 2 * 512 * 512 * 512
 
@@ -72,13 +73,15 @@ def tile_picked_simkgpairwindfold_none_p_kernel(
         for win in s_win + w_win:
             nc.scalar.copy(win[:, S:], zero[:].to_broadcast([P, S]))
 
+        sign_or_zero = sbuf("sign_or_zero", PLANES, F32)
         sign = sbuf("sign", PLANES, F32)
         ga_abs = sbuf("ga_abs", PLANES, F32)
         gb_signed = sbuf("gb_signed", PLANES, F32)
-        nc.gpsimd.tensor_scalar(sign[:], ga_keys[:], 0.0, 2.0, ALU.is_ge, ALU.mult)
-        nc.gpsimd.tensor_scalar(sign[:], sign[:], -1.0, 1.0, ALU.add, ALU.mult)
-        nc.gpsimd.tensor_tensor(ga_abs[:], ga_keys[:], sign[:], ALU.mult)
-        nc.gpsimd.tensor_tensor(gb_signed[:], gb_keys[:], sign[:], ALU.mult)
+        nc.scalar.activation(sign_or_zero[:], ga_keys[:], ACT.Sign)
+        nc.scalar.activation(ga_abs[:], ga_keys[:], ACT.Abs)
+        nc.scalar.activation(sign[:], sign_or_zero[:], ACT.Sign, bias=0.5)
+        for t in range(PLANES):
+            nc.scalar.activation(gb_signed[:, t : t + 1], gb_keys[:, t : t + 1], ACT.Copy, scale=sign[:, t : t + 1])
 
         d_scale_picked = sbuf("d_scale_picked", S, U8)
         x_scale_picked = sbuf("x_scale_picked", S, U8)
@@ -192,9 +195,9 @@ def tile_picked_simkgpairwindfold_none_p_kernel(
         def weave_z(h, u, members, summed):
             woven = sbuf("z_woven%d_%d" % (h, u), S, BF16)
             nc.vector.tensor_tensor(
-                woven[:].rearrange("p (c i t) -> p c t i", i=WEAVE, t=PLANES),
-                summed[:].rearrange("p (t c i) -> p c t i", i=WEAVE, t=PLANES),
-                members[:].rearrange("p (t u c i e) -> p u e c t i", t=PLANES, u=2, i=WEAVE, e=2)[:, u, 0],
+                woven[:].rearrange("p (c i t) -> p c t i", i=WEAVE_Z, t=PLANES),
+                summed[:].rearrange("p (t c i) -> p c t i", i=WEAVE_Z, t=PLANES),
+                members[:].rearrange("p (t u c i e) -> p u e c t i", t=PLANES, u=2, i=WEAVE_Z, e=2)[:, u, 0],
                 ALU.min,
             )
             return woven

@@ -93,18 +93,22 @@ def tile_picked_simkgpairwindfold_none_p_kernel(
             d_scale_picked[:].rearrange("p (c i t) -> p c t i", t=PLANES, i=LINE),
         )
         nc.vector.tensor_copy(scale_rows[:, S:].bitcast(I32), x_scale_picked[:].bitcast(I32))
-        for r in range(1, 4):
-            nc.sync.dma_start(scale_rows[r:P:32, :].bitcast(I32), scale_rows[8 * r : P : 32, :].bitcast(I32))
+        for r, queue in ((1, nc.sync), (2, nc.scalar), (3, nc.sync)):
+            queue.dma_start(scale_rows[r:P:32, :].bitcast(I32), scale_rows[8 * r : P : 32, :].bitcast(I32))
 
         d_picked = sbuf("d_picked", S, U32)
         x_picked = sbuf("x_picked", S, U32)
         d_dealt = sbuf("d_dealt", S, U32)
         nc.vector.tensor_copy(d_picked[:], d_word_table[:].bitcast(U32).indirect(kidx_list[:]))
-        nc.vector.tensor_copy(x_picked[:], x_word_table[:].bitcast(U32).indirect(offs_list[:]))
         nc.vector.tensor_copy(
             d_dealt[:].rearrange("p (t c i) -> p c t i", t=PLANES, i=LINE // 4),
             d_picked[:].rearrange("p (c i t) -> p c t i", t=PLANES, i=LINE // 4),
         )
+        for h in range(2):
+            nc.vector.tensor_copy(
+                x_picked[:, h * HALF : (h + 1) * HALF],
+                x_word_table[:].bitcast(U32).indirect(offs_list[:, h * HALF // 16 : (h + 1) * HALF // 16]),
+            )
 
         def first_product(bank, t, tokens):
             keys = slice(t * P, (t + 1) * P)

from contextlib import ExitStack

import concourse.mybir as mybir

F32 = mybir.dt.float32
BF16 = mybir.dt.bfloat16
I32 = mybir.dt.int32
U32 = mybir.dt.uint32
U16 = mybir.dt.uint16
U8 = mybir.dt.uint8
FP8X4 = mybir.dt.float8_e4m3fn_x4
ALU = mybir.AluOpType
ACT = mybir.ActivationFunctionType

P = 128
PLANES = 4
TABLE = 2048
S = 512
HALF = S // 2
PAIRS = 256
LINE = 16
WEAVE = 4
WEAVE_Z = 2
SIXTEENTH = 0.0625
FLOPS = 2 * 2 * 512 * 512 * 512


def tile_picked_simkgpairwindfold_none_p_kernel(
    tc, x_words, x_scales, d_words, d_scales, ga, gb, offs, kidx, n1, n2, n3, n4, n5, out
):
    nc = tc.nc
    with ExitStack() as ctx:
        keep = ctx.enter_context(tc.tile_pool(name="keep", bufs=1))
        psum = ctx.enter_context(tc.psum_pool(name="psum", bufs=1))

        def sbuf(name, cols, dtype, slot=None):
            return keep.tile([P, cols], dtype, name=name, tag=slot or name, align_bytes=64)

        def load_list(name, src):
            offsets = keep.tile(list(src.shape), U16, name=name)
            nc.sync.dma_start(offsets[:], src)
            return offsets

        d_scale_table = sbuf("d_scale_table", TABLE, U8)
        x_scale_table = sbuf("x_scale_table", TABLE, U8)
        for table in (d_scale_table, x_scale_table):
            nc.vector.memset(table[:, 0 : TABLE // 2].bitcast(I32), 0)
            nc.gpsimd.memset(table[:, TABLE // 2 :].bitcast(I32), 0)
        d_word_table = sbuf("d_word_table", TABLE, I32)
        x_word_table = sbuf("x_word_table", TABLE, I32)
        ga_keys = sbuf("ga_keys", PLANES, F32)
        gb_keys = sbuf("gb_keys", PLANES, F32)
        kidx_list = load_list("kidx_list", kidx)
        offs_list = load_list("offs_list", offs)
        nc.sync.dma_start(ga_keys[:], ga.rearrange("(p t) o -> p (t o)", t=PLANES))
        nc.sync.dma_start(gb_keys[:], gb.rearrange("(p t) o -> p (t o)", t=PLANES))
        n3_list = load_list("n3_list", n3)
        nc.sync.dma_start(d_scale_table[0:P:8, :].bitcast(I32), d_scales[0].bitcast(I32))
        nc.sync.dma_start(x_scale_table[0:P:8, :].bitcast(I32), x_scales[0].bitcast(I32))
        nc.sync.dma_start(d_word_table[:], d_words[0].rearrange("p n t -> p (n t)").bitcast(I32))
        nc.sync.dma_start(x_word_table[:], x_words[0].rearrange("p n t -> p (n t)").bitcast(I32))
        n2_list = load_list("n2_list", n2)
        n1_list = load_list("n1_list", n1)
        n5_list = load_list("n5_list", n5)
        n4_list = load_list("n4_list", n4)

        zero = sbuf("zero", 1, F32)
        nc.vector.memset(zero[:], 0.0)
        warm_up = sbuf("warm_up", 1, F32)
        nc.scalar.activation(warm_up[:], zero[:], ACT.Sigmoid)
        s_win = [sbuf("s_win%d" % t, 2 * S, F32) for t in range(PLANES)]
        w_win = [sbuf("w_win%d" % t, 2 * S, F32) for t in range(PLANES)]
        for win in s_win + w_win:
            nc.scalar.copy(win[:, S:], zero[:].to_broadcast([P, S]))

        sign_or_zero = sbuf("sign_or_zero", PLANES, F32)
        sign = sbuf("sign", PLANES, F32)
        ga_abs = sbuf("ga_abs", PLANES, F32)
        gb_signed = sbuf("gb_signed", PLANES, F32)
        nc.scalar.activation(sign_or_zero[:], ga_keys[:], ACT.Sign)
        nc.scalar.activation(ga_abs[:], ga_keys[:], ACT.Abs)
        nc.scalar.activation(sign[:], sign_or_zero[:], ACT.Sign, bias=0.5)
        for t in range(PLANES):
            nc.scalar.activation(gb_signed[:, t : t + 1], gb_keys[:, t : t + 1], ACT.Copy, scale=sign[:, t : t + 1])

        d_scale_picked = sbuf("d_scale_picked", S, U8)
        x_scale_picked = sbuf("x_scale_picked", S, U8)
        nc.vector.tensor_copy(d_scale_picked[:], d_scale_table[:].indirect(kidx_list[:]))
        nc.vector.tensor_copy(x_scale_picked[:], x_scale_table[:].indirect(offs_list[:]))
        scale_rows = sbuf("scale_rows", 2 * S, U8)
        nc.vector.tensor_copy(
            scale_rows[:, 0:S].rearrange("p (t c i) -> p c t i", t=PLANES, i=LINE),
            d_scale_picked[:].rearrange("p (c i t) -> p c t i", t=PLANES, i=LINE),
        )
        nc.vector.tensor_copy(scale_rows[:, S:].bitcast(I32), x_scale_picked[:].bitcast(I32))
        for r, queue in ((1, nc.sync), (2, nc.scalar), (3, nc.sync)):
            queue.dma_start(scale_rows[r:P:32, :].bitcast(I32), scale_rows[8 * r : P : 32, :].bitcast(I32))

        d_picked = sbuf("d_picked", S, U32)
        x_picked = sbuf("x_picked", S, U32)
        d_dealt = sbuf("d_dealt", S, U32)
        nc.vector.tensor_copy(d_picked[:], d_word_table[:].bitcast(U32).indirect(kidx_list[:]))
        nc.vector.tensor_copy(
            d_dealt[:].rearrange("p (t c i) -> p c t i", t=PLANES, i=LINE // 4),
            d_picked[:].rearrange("p (c i t) -> p c t i", t=PLANES, i=LINE // 4),
        )
        for h in range(2):
            nc.vector.tensor_copy(
                x_picked[:, h * HALF : (h + 1) * HALF],
                x_word_table[:].bitcast(U32).indirect(offs_list[:, h * HALF // 16 : (h + 1) * HALF // 16]),
            )

        def first_product(bank, t, tokens):
            keys = slice(t * P, (t + 1) * P)
            nc.tensor.matmul_mx(
                out=bank,
                lhsT=d_dealt[:, keys].bitcast(FP8X4),
                lhsT_scale=scale_rows[:, keys],
                rhs=x_picked[:, tokens].bitcast(FP8X4),
                rhs_scale=scale_rows[:, S + tokens.start : S + tokens.stop],
                start=True,
                stop=True,
            )

        left, right, every = slice(0, HALF), slice(HALF, S), slice(0, S)
        s_banks = [psum.tile([P, S], F32, name="s_bank%d" % t) for t in range(PLANES)]
        right_bank = psum.tile([P, S], F32, name="cm_bank3")
        first_product(s_banks[0][:, left], 0, left)
        first_product(right_bank[:, left], 0, right)
        for t in range(1, PLANES):
            first_product(s_banks[t][:], t, every)
        nc.scalar.mul(s_win[0][:, left], s_banks[0][:, left], SIXTEENTH)
        nc.vector.tensor_scalar_mul(s_win[0][:, right], right_bank[:, left], SIXTEENTH)
        for t in (1, 2):
            nc.vector.tensor_scalar_mul(s_win[t][:, every], s_banks[t][:], SIXTEENTH)

        last = PLANES - 1
        z2_planes = sbuf("z2_planes", PLANES * S, BF16, "first_less_s0")
        for t in range(PLANES):
            if t == last:
                nc.scalar.mul(s_win[t][:, every], s_banks[t][:], SIXTEENTH)
            else:
                nc.vector.tensor_scalar_mul(w_win[t][:, every], s_win[t][:, every], ga_abs[:, t : t + 1])
            at_n3 = sbuf("at_n3_%d" % t, S, F32)
            diff = sbuf("diff%d" % t, S, F32)
            nc.scalar.activation(at_n3[:], s_win[t][:].indirect(n3_list[:]), ACT.Copy)
            if t == last:
                nc.scalar.activation(w_win[t][:, every], s_win[t][:, every], ACT.Copy, scale=ga_abs[:, t : t + 1])
            nc.vector.tensor_tensor(diff[:], s_win[t][:].indirect(n2_list[:]), at_n3[:], ALU.subtract)
            nc.vector.scalar_tensor_tensor(
                z2_planes[:, t * S : (t + 1) * S],
                s_win[t][:, every],
                gb_signed[:, t : t + 1],
                diff[:],
                ALU.mult,
                ALU.mult,
            )
        z2_codes = sbuf("z2_codes", S, U32)
        z2_scale = sbuf("z2_scale", S, U8)
        z2_woven = [sbuf("z2_woven%d" % h, PLANES * HALF, BF16) for h in range(2)]
        for h in range(2):
            nc.vector.tensor_copy(
                z2_woven[h][:].rearrange("p (c i t) -> p c t i", i=WEAVE, t=PLANES),
                z2_planes[:].rearrange("p (t h c i) -> p h c t i", t=PLANES, h=2, i=WEAVE)[:, h],
            )
        for h, cols in enumerate((left, right)):
            nc.vector.quantize_mx(out=z2_codes[:, cols].bitcast(FP8X4), scales=z2_scale[:, cols], in_=z2_woven[h][:])

        def gather_members(h, slot):
            members = sbuf("members%d" % h, PLANES * S, F32, slot)
            entries = n1_list[:, h * S // 16 : (h + 1) * S // 16]
            for t in range(PLANES):
                nc.scalar.activation(members[:, t * S : (t + 1) * S], w_win[t][:].indirect(entries), ACT.Copy)
            return members

        def first_less_s(h, members):
            less = sbuf("first_less_s%d" % h, PLANES * HALF, F32)
            for t in range(PLANES):
                nc.vector.tensor_tensor(
                    less[:, t * HALF : (t + 1) * HALF],
                    members[:, t * S : (t + 1) * S : 2],
                    w_win[t][:, h * HALF : (h + 1) * HALF],
                    ALU.subtract,
                )
            return less

        def plus_second(h, u, members, less, slot):
            summed = sbuf("summed%d_%d" % (h, u), S, F32, slot)
            nc.vector.scalar_tensor_tensor(
                summed[:].rearrange("p (t c) -> p t c", t=PLANES),
                less[:].rearrange("p (t u c) -> p u t c", t=PLANES, u=2)[:, u],
                0.0,
                members[:].rearrange("p (t u c e) -> p u e t c", t=PLANES, u=2, e=2)[:, u, 1],
                ALU.min,
                ALU.add,
            )
            return summed

        def weave_z(h, u, members, summed):
            woven = sbuf("z_woven%d_%d" % (h, u), S, BF16)
            nc.vector.tensor_tensor(
                woven[:].rearrange("p (c i t) -> p c t i", i=WEAVE_Z, t=PLANES),
                summed[:].rearrange("p (t c i) -> p c t i", i=WEAVE_Z, t=PLANES),
                members[:].rearrange("p (t u c i e) -> p u e c t i", t=PLANES, u=2, i=WEAVE_Z, e=2)[:, u, 0],
                ALU.min,
            )
            return woven

        def second_product(m, woven):
            codes = sbuf("z_codes%d" % m, P, U32)
            scale = sbuf("z_scale%d" % m, P, U8)
            nc.vector.quantize_mx(out=codes[:].bitcast(FP8X4), scales=scale[:], in_=woven[:])
            bank = psum.tile([P, S], F32, name="cm_bank%d" % m)
            nc.tensor.matmul_mx(
                out=bank[:],
                lhsT=codes[:].bitcast(FP8X4),
                lhsT_scale=scale[:],
                rhs=z2_codes[:].bitcast(FP8X4),
                rhs_scale=z2_scale[:],
                start=True,
                stop=True,
            )
            return bank

        def empty_bank(m, bank, scale_by):
            cm = sbuf("cm%d" % m, S, F32)
            scale_by(cm[:], bank[:], SIXTEENTH)
            return cm

        def gate_of(m, cm):
            gate = sbuf("gate%d" % m, PAIRS, F32)
            nc.scalar.activation(gate[:], cm[:].indirect(n5_list[:]), ACT.Sigmoid)
            return gate

        def store(m, cm):
            nc.sync.dma_start(out[m * P : (m + 1) * P, :], cm[:])

        members = [gather_members(0, None), gather_members(1, "at_n3_%d" % last)]

        less = first_less_s(0, members[0])
        summed = [plus_second(0, 0, members[0], less, None), plus_second(0, 1, members[0], less, "first_less_s1")]
        woven = [weave_z(0, u, members[0], summed[u]) for u in range(2)]
        banks = [second_product(u, woven[u]) for u in range(2)]
        cms, gates = [], []
        for m in (0, 1):
            cms.append(empty_bank(m, banks[m], nc.scalar.mul))
            gates.append(gate_of(m, cms[m]))

        less = first_less_s(1, members[1])
        summed = [plus_second(1, u, members[1], less, None) for u in range(2)]
        woven = [weave_z(1, u, members[1], summed[u]) for u in range(2)]

        ra0 = sbuf("ra0", PAIRS, F32, "summed1_0")
        pa1 = sbuf("pa1", PAIRS, F32, "summed1_1")
        banks.append(second_product(2, woven[0]))
        nc.vector.tensor_tensor(ra0[:], cms[0][:].indirect(n4_list[:]), gates[0][:], ALU.mult)
        banks.append(second_product(3, woven[1]))
        nc.scalar.activation(pa1[:], cms[1][:].indirect(n4_list[:]), ACT.Copy)
        nc.scalar.activation(cms[0][:].indirect(n5_list[:]), ra0[:], ACT.Copy)
        nc.vector.tensor_tensor(cms[1][:].indirect(n5_list[:]), pa1[:], gates[1][:], ALU.mult)
        for m in (0, 1):
            store(m, cms[m])

        cms.append(empty_bank(2, banks[2], nc.scalar.mul))
        cms.append(empty_bank(3, banks[3], nc.vector.tensor_scalar_mul))
        gates.extend([gate_of(m, cms[m]) for m in (2, 3)])
        pa3 = sbuf("pa3", PAIRS, F32)
        ra2 = sbuf("ra2", PAIRS, F32)
        nc.vector.tensor_copy(pa3[:], cms[3][:].indirect(n4_list[:]))
        nc.vector.tensor_tensor(ra2[:], cms[2][:].indirect(n4_list[:]), gates[2][:], ALU.mult)
        nc.scalar.activation(cms[2][:].indirect(n5_list[:]), ra2[:], ACT.Copy)
        nc.vector.tensor_tensor(cms[3][:].indirect(n5_list[:]), pa3[:], gates[3][:], ALU.mult)
        for m in (2, 3):
            store(m, cms[m])
